import numpy as np
import ml_dtypes


def mxq(x, axis, fmt="e4m3"):
    dtype, down = {"e4m3": (ml_dtypes.float8_e4m3fn, 7), "e5m2": (ml_dtypes.float8_e5m2, 14)}[fmt]
    v = np.moveaxis(np.asarray(x, np.float32).astype(ml_dtypes.bfloat16).astype(np.float64), axis, -1)
    blocks = v.reshape(v.shape[:-1] + (-1, 32))
    amax = np.abs(blocks).max(-1, keepdims=True)
    byte = np.maximum(np.where(amax > 0, np.frexp(amax)[1] - 1 + 127, 0) - down, 1)
    scale = np.exp2(byte - 127.0)
    codes = (blocks / scale).astype(np.float32).astype(dtype).astype(np.float64)
    return np.moveaxis((codes * scale).reshape(v.shape), -1, axis)


WIDE = False


def mx_kscale(k):
    if not WIDE:
        return np.ones(k)
    levels = np.array([10, -10, 5, -5, 0])
    if k % 512:
        return np.exp2(np.random.permutation(np.resize(levels, k // 32))).repeat(32)
    a = np.empty((k // 512, 16))
    for p in range(k // 512):
        a[p, :8] = np.random.permutation(np.resize(levels, 8))
        for g in range(8):
            far = levels[np.abs(levels - a[p, g]) >= 10]
            a[p, g + 8] = far[np.random.randint(len(far))]
    return np.exp2(a.ravel()).repeat(32)


def f64(x):
    return np.asarray(x).astype(np.float64)


def striped(idx):
    return np.tile(idx.reshape(-1, 16).T, (8, 1)).astype(np.uint16)


def unstriped(offs):
    return offs[:16].T.reshape(-1).astype(np.int64)


E2M1 = np.array([0.0, 0.5, 1.0, 1.5, 2.0, 3.0, 4.0, 6.0, -0.0, -0.5, -1.0, -1.5, -2.0, -3.0, -4.0, -6.0])


def pack_weight(w, fmt):
    k, n = w.shape
    w = f64(np.asarray(w, np.float32).astype(ml_dtypes.bfloat16)).reshape(k // 32, 32, n)
    amax = np.abs(w).max(1)
    if fmt == "e4m3":
        byte = np.frexp(amax)[1] - 1 + 127 - 7
    else:
        mant, ex = np.frexp(amax / 6.0)
        byte = np.where(mant > 0.5, ex, ex - 1) + 127
    byte = np.clip(np.where(amax > 0, byte, 1), 1, 254)
    scaled = (w * np.exp2(127.0 - byte)[:, None, :]).reshape(k, n).astype(np.float32)
    by_word = np.ascontiguousarray(scaled.reshape(k // 512, 128, 4, n).transpose(0, 1, 3, 2))
    if fmt == "e4m3":
        words = by_word.astype(ml_dtypes.float8_e4m3fn).view(np.uint8)
    else:
        c = by_word.astype(ml_dtypes.float4_e2m1fn).view(np.uint8) & 0xF
        words = (c[..., 0::2] | (c[..., 1::2] << 4)).reshape(k // 512, 128, 2 * n)
    return np.ascontiguousarray(words), np.ascontiguousarray(byte.astype(np.uint8).reshape(k // 512, 16, n))


def unpack_weight(words, scales, fmt):
    g, _, n = scales.shape
    words = np.ascontiguousarray(words).reshape(g, 128, n, -1)
    if fmt == "e4m3":
        vals = words.view(ml_dtypes.float8_e4m3fn).astype(np.float64)
    else:
        nib = np.empty((g, 128, n, 4), np.uint8)
        nib[..., 0::2] = words & 0xF
        nib[..., 1::2] = words >> 4
        vals = E2M1[nib]
    vals = vals * np.repeat(np.exp2(scales.astype(np.float64) - 127.0), 8, axis=1)[..., None]
    return vals.transpose(0, 1, 3, 2).reshape(g * 512, n)


def silu(v):
    return v / (1.0 + np.exp(-np.maximum(v, -700.0)))


K, T, E, C, H, N = 1024, 768, 4, 256, 512, 128
PAD = 32


def by_expert(wq, xq):
    return np.concatenate([wq[e].T @ xq[:, e * C:(e + 1) * C] for e in range(E)], axis=1)


def setup_inputs():
    n = np.random.standard_normal
    s = mx_kscale(K)[:, None]
    u = mx_kscale(H)
    first = np.random.permutation(np.repeat(np.arange(E), T // E))
    second = (first + 1 + np.random.permutation(np.repeat(np.arange(E - 1), -(-T // (E - 1)))[:T])) % E
    while np.bincount(second, minlength=E).max() != T // E:
        load = np.bincount(second, minlength=E); hi, lo = int(load.argmax()), int(load.argmin())
        t = np.flatnonzero((second == hi) & (first != lo))[0]; second[t] = lo
    slot_token = np.empty(E * C, np.int64); pos = np.empty((2, T), np.int64); fill = np.zeros(E, np.int64)
    place = np.stack([np.random.permutation(C) for _ in range(E)])
    for r, deal in enumerate((first, second)):
        for t in np.random.permutation(T):
            e = deal[t]
            if fill[e] < C: j = e * C + place[e, fill[e]]; fill[e] += 1; slot_token[j] = t; pos[r, t] = j
            else: pos[r, t] = E * C + t % PAD
    g = np.random.uniform(0.2, 0.8, T)
    w1 = [pack_weight(m, "e2m1") for m in n((E, K, H)) / np.sqrt(K) / s[None]]
    w3 = [pack_weight(m, "e2m1") for m in n((E, K, H)) / np.sqrt(K) / s[None] * u[None, None, :]]
    w2 = [pack_weight(m, "e2m1") for m in n((E, H, N)) / np.sqrt(H) / u[None, :, None]]
    return {
        "xT": (n((K, T)) * s).astype(np.float32),
        "w1_words": np.stack([m[0] for m in w1]),
        "w1_scales": np.stack([m[1] for m in w1]),
        "w3_words": np.stack([m[0] for m in w3]),
        "w3_scales": np.stack([m[1] for m in w3]),
        "w2_words": np.stack([m[0] for m in w2]),
        "w2_scales": np.stack([m[1] for m in w2]),
        "gate": np.stack([np.tile(g, (N, 1)), np.tile(1.0 - g, (N, 1))]).astype(np.float32),
        "offs": striped(slot_token),
        "pos1": striped(pos[0]),
        "pos2": striped(pos[1]),
    }


def reference(xT, w1_words, w1_scales, w3_words, w3_scales, w2_words, w2_scales, gate, offs, pos1, pos2):
    idx = unstriped(offs)
    w1 = np.stack([unpack_weight(w1_words[e], w1_scales[e], "e2m1") for e in range(E)])
    w3 = np.stack([unpack_weight(w3_words[e], w3_scales[e], "e2m1") for e in range(E)])
    w2 = np.stack([unpack_weight(w2_words[e], w2_scales[e], "e2m1") for e in range(E)])
    xq = mxq(f64(xT)[:, idx], 0, "e4m3")
    h = silu(by_expert(w1, xq))
    h = h * by_expert(w3, xq)
    y = by_expert(w2, mxq(h, 0, "e4m3"))
    y = np.concatenate([y, np.zeros((N, PAD))], axis=1)
    return f64(gate[0]) * y[:, unstriped(pos1)] + f64(gate[1]) * y[:, unstriped(pos2)]

@@ -1,0 +1,293 @@
+from contextlib import ExitStack
+
+import concourse.mybir as mybir
+from concourse.masks import make_identity
+
+F32 = mybir.dt.float32
+BF16 = mybir.dt.bfloat16
+I32 = mybir.dt.int32
+U32 = mybir.dt.uint32
+U16 = mybir.dt.uint16
+U8 = mybir.dt.uint8
+FP8X4 = mybir.dt.float8_e4m3fn_x4
+FP4X4 = mybir.dt.float4_e2m1fn_x4
+MULT = mybir.AluOpType.mult
+ADD = mybir.AluOpType.add
+COPY = mybir.ActivationFunctionType.Copy
+SILU = mybir.ActivationFunctionType.Silu
+
+K, T, E, C, H, N = 1024, 768, 4, 256, 512, 128
+S = E * C
+PAD = 32
+P = 128
+PASSES = K // 512
+G = S // P
+
+FLOPS = 2 * S * (2 * K * H + H * N)
+
+X_CHUNKS = (((0, 512), (512, 256)), ((0, 256), (256, 256), (512, 256)))
+V_SHARE = {(0, 0): 288, (0, 512): 160}
+Q_CHUNKS = (((0, 512), (512, 256)), ((0, 256), (256, 256), (512, 256)))
+
+
+def tile_moe_cap2_glu_silu_kernel(tc, xT, w1_words, w1_scales, w3_words, w3_scales, w2_words, w2_scales, gate, offs, pos1, pos2, out):
+    nc = tc.nc
+    with ExitStack() as ctx:
+        keep = ctx.enter_context(tc.tile_pool(name="keep", bufs=1))
+        work = ctx.enter_context(tc.tile_pool(name="work", bufs=4))
+        banks = ctx.enter_context(tc.psum_pool(name="banks", bufs=8))
+
+        offs_t = keep.tile([P, S // 16], U16, name="offs_t")
+        pos1_t = keep.tile([P, T // 16], U16, name="pos1_t")
+        pos2_t = keep.tile([P, T // 16], U16, name="pos2_t")
+
+        w1_sc = keep.tile([P, E * PASSES, H], U8, name="w1_sc", align_bytes=64)
+        w3_sc = keep.tile([P, E * PASSES, H], U8, name="w3_sc", align_bytes=64)
+        w2_sc = keep.tile([P, E, N], U8, name="w2_sc", align_bytes=64)
+        w1_wd = keep.tile([P, E, PASSES, 2 * H], U8, name="w1_wd", align_bytes=64)
+        w3_wd = keep.tile([P, E, PASSES, 2 * H], U8, name="w3_wd", align_bytes=64)
+        w2_wd = keep.tile([P, E, 2 * N], U8, name="w2_wd", align_bytes=64)
+        gates = keep.tile([P, 2, T], F32, name="gates")
+
+        x_raw = {}
+        x_grp = []
+        x_codes = []
+        x_bytes = []
+        g_codes = []
+        g_bytes = []
+        for s in range(PASSES):
+            for c0, w in X_CHUNKS[s]:
+                x_raw[s, c0] = keep.tile([P, 4, w], F32, name=f"x_raw{s}_{c0}")
+            x_grp.append(keep.tile([P, T, 4], BF16, name=f"x_grp{s}", align_bytes=64))
+            x_codes.append(keep.tile([P, T], U32, name=f"x_codes{s}", align_bytes=64))
+            x_bytes.append(keep.tile([P, T], U8, name=f"x_bytes{s}", align_bytes=64))
+            g_codes.append(keep.tile([P, S], U32, name=f"g_codes{s}", align_bytes=64))
+            g_bytes.append(keep.tile([P, S], U8, name=f"g_bytes{s}", align_bytes=64))
+        y_all = keep.tile([P, S + PAD], F32, name="y_all")
+        ident = keep.tile([P, P], F32, name="ident")
+        warm = keep.tile([P, 1], F32, name="warm")
+
+        nc.vector.memset(warm[:], 0.0)
+        nc.scalar.activation(out=warm[:], in_=warm[:], func=SILU)
+        nc.vector.memset(w1_sc[:].rearrange("p a b -> p (a b)").bitcast(I32), 0)
+        nc.gpsimd.memset(w3_sc[:].rearrange("p a b -> p (a b)").bitcast(I32), 0)
+        nc.gpsimd.memset(x_bytes[0][:].bitcast(I32), 0)
+
+        def load_x(s, c0, w):
+            rows = xT[512 * s : 512 * (s + 1), c0 : c0 + w].rearrange("(p j) c -> p j c", j=4)
+            nc.sync.dma_start(out=x_raw[s, c0][:], in_=rows)
+
+        def load_words(e):
+            for tile, words in ((w1_wd, w1_words), (w3_wd, w3_words)):
+                nc.sync.dma_start(
+                    out=tile[:, e].bitcast(I32),
+                    in_=words[e].rearrange("s p b -> p s b").bitcast(I32),
+                )
+
+        def load_scales(queue, tile, scales):
+            for q in range(4):
+                queue.dma_start(
+                    out=tile[32 * q : 32 * q + 4].bitcast(I32),
+                    in_=scales[:, :, 4 * q : 4 * q + 4, :].rearrange("e s r i -> r (e s) i").bitcast(I32),
+                )
+
+        def load_w2():
+            nc.sync.dma_start(
+                out=w2_wd[:].bitcast(I32), in_=w2_words.rearrange("e s p b -> p (e s) b").bitcast(I32)
+            )
+
+        def load_x_pass(s):
+            for c0, w in X_CHUNKS[s]:
+                load_x(s, c0, w)
+
+        load_x_pass(0)
+        nc.sync.dma_start(out=offs_t[:], in_=offs)
+        load_scales(nc.sync, w1_sc, w1_scales)
+        load_scales(nc.gpsimd, w3_sc, w3_scales)
+        nc.gpsimd.memset(x_bytes[1][:].bitcast(I32), 0)
+        nc.gpsimd.memset(w2_sc[:].rearrange("p a b -> p (a b)").bitcast(I32), 0)
+        nc.gpsimd.memset(y_all[:, S:], 0.0)
+        make_identity(nc, ident[:])
+        load_scales(nc.gpsimd, w2_sc, w2_scales)
+        load_words(0)
+        load_x_pass(1)
+        for e in range(1, E):
+            load_words(e)
+        load_w2()
+        nc.sync.dma_start(out=pos1_t[:], in_=pos1)
+        nc.sync.dma_start(out=pos2_t[:], in_=pos2)
+        nc.sync.dma_start(out=gates[:], in_=gate.rearrange("r p t -> p r t"))
+
+        def cast_x(s, c0, w):
+            src = x_raw[s, c0][:].rearrange("p j c -> p c j")
+            v = V_SHARE.get((s, c0), 0)
+            if v:
+                nc.vector.tensor_copy(out=x_grp[s][:, c0 : c0 + v, :], in_=src[:, 0:v, :])
+            if v < w:
+                nc.scalar.activation(out=x_grp[s][:, c0 + v : c0 + w, :], in_=src[:, v:w, :], func=COPY)
+
+        def quantize_x(s, c0, w):
+            nc.vector.quantize_mx(
+                out=x_codes[s][:, c0 : c0 + w].bitcast(FP8X4),
+                scales=x_bytes[s][:, c0 : c0 + w],
+                in_=x_grp[s][:, c0 : c0 + w, :].rearrange("p c j -> p (c j)"),
+            )
+
+        def gather(s, e, n):
+            slots = slice(C * e, C * (e + n))
+            lst = offs_t[:, 16 * e : 16 * (e + n)]
+            nc.vector.tensor_copy(out=g_codes[s][:, slots], in_=x_codes[s][:].indirect(lst))
+            nc.vector.tensor_copy(out=g_bytes[s][:, slots], in_=x_bytes[s][:].indirect(lst))
+
+        ab = {}
+
+        def product(g, s):
+            e = g // 2
+            cols = slice(P * g, P * (g + 1))
+            for m, wd, sc in ((0, w1_wd, w1_sc), (1, w3_wd, w3_sc)):
+                if s == 0:
+                    ab[g, m] = banks.tile([P, H], F32, name="bank")
+                nc.tensor.matmul_mx(
+                    out=ab[g, m][:],
+                    lhsT=g_codes[s][:, cols].bitcast(FP8X4),
+                    lhsT_scale=g_bytes[s][:, cols],
+                    rhs=wd[:, e, s, :].bitcast(FP4X4),
+                    rhs_scale=sc[:, PASSES * e + s, :],
+                    start=(s == 0),
+                    stop=(s == PASSES - 1),
+                )
+
+        sil = {}
+        hid = {}
+
+        def activate(g):
+            sil[g] = work.tile([P, H], F32, name="sil")
+            nc.scalar.activation(
+                out=sil[g][:].rearrange("p (u m d) -> p u m d", u=2, d=2),
+                in_=ab[g, 0][:].rearrange("p (m u d) -> p u m d", u=2, d=2),
+                func=SILU,
+            )
+
+        def multiply(g):
+            hid[g] = work.tile([P, H], BF16, name="hid")
+            nc.vector.tensor_tensor(
+                out=hid[g][:].rearrange("p (u m d) -> p u m d", u=2, d=2),
+                in0=ab[g, 1][:].rearrange("p (m u d) -> p u m d", u=2, d=2),
+                in1=sil[g][:].rearrange("p (u m d) -> p u m d", u=2, d=2),
+                op=MULT,
+            )
+
+        def turn(bank, half, g):
+            words = hid[g][:].bitcast(F32)
+            for u in range(2):
+                nc.tensor.transpose(bank[:, half, u, :], words[:, P * u : P * (u + 1)], ident[:])
+
+        def unload(engine_copy, bank, n):
+            grouped = work.tile([P, C, 4], BF16, name="grouped", align_bytes=64)
+            engine_copy(
+                out=grouped[:, 0 : P * n, :].rearrange("p c t -> p (c t)").bitcast(F32).rearrange("p (a c u) -> p a c u", a=n, u=2),
+                in_=bank[:, 0:n, :, :].rearrange("p a u c -> p a c u"),
+            )
+            return grouped
+
+        def second(grouped, e, c0, w):
+            h_codes = work.tile([P, C], U32, name="h_codes", align_bytes=64)
+            h_bytes = work.tile([P, C], U8, name="h_bytes", align_bytes=64)
+            nc.vector.quantize_mx(
+                out=h_codes[:, 0:w].bitcast(FP8X4),
+                scales=h_bytes[:, 0:w],
+                in_=grouped[:, 0:w, :].rearrange("p c t -> p (c t)"),
+            )
+            y = banks.tile([P, H], F32, name="bank")
+            nc.tensor.matmul_mx(
+                out=y[:, 0:w],
+                lhsT=w2_wd[:, e, :].bitcast(FP4X4),
+                lhsT_scale=w2_sc[:, e, :],
+                rhs=h_codes[:, 0:w].bitcast(FP8X4),
+                rhs_scale=h_bytes[:, 0:w],
+                start=True,
+                stop=True,
+            )
+            nc.scalar.copy(out=y_all[:, c0 : c0 + w], in_=y[:, 0:w])
+
+        for c0, w in X_CHUNKS[0]:
+            cast_x(0, c0, w)
+        for c0, w in Q_CHUNKS[0]:
+            quantize_x(0, c0, w)
+        early = 3
+        gather(0, 0, 1)
+        gather(0, 1, 1)
+        for g in range(early):
+            product(g, 0)
+        for c0, w in X_CHUNKS[1]:
+            cast_x(1, c0, w)
+        gather(0, 2, 2)
+        for c0, w in Q_CHUNKS[1]:
+            quantize_x(1, c0, w)
+
+        def stage_one(g):
+            if g >= early:
+                product(g, 0)
+            product(g, 1)
+            activate(g)
+
+        grouped = {}
+
+        def middle(e):
+            bank = banks.tile([P, 2, 2, P], F32, name="bank")
+            for half in range(2):
+                multiply(2 * e + half)
+                turn(bank, half, 2 * e + half)
+            grouped[e] = unload(nc.scalar.copy, bank, 2)
+
+        def finish_expert(e):
+            second(grouped[e], e, C * e, C)
+
+        gather(1, 0, 1)
+        stage_one(0)
+        stage_one(1)
+        gather(1, 1, 1)
+        stage_one(2)
+        stage_one(3)
+        gather(1, 2, 2)
+        middle(0)
+        stage_one(4)
+        stage_one(5)
+        middle(1)
+        finish_expert(0)
+        stage_one(6)
+        stage_one(7)
+        middle(2)
+        finish_expert(1)
+        last = []
+        for half, engine_copy in ((0, nc.scalar.copy), (1, nc.vector.tensor_copy)):
+            g = G - 2 + half
+            bank = banks.tile([P, 2, 2, P], F32, name="bank")
+            multiply(g)
+            turn(bank, 0, g)
+            last.append((engine_copy, bank, g))
+        finish_expert(2)
+        for engine_copy, bank, g in last:
+            part = unload(engine_copy, bank, 1)
+            second(part, E - 1, P * g, P)
+
+        picked = {}
+        pieces = ((0, 256), (256, 256), (512, 256))
+        for i, (t0, w) in enumerate(pieces):
+            for r, lst in ((0, pos1_t), (1, pos2_t)):
+                picked[i, r] = keep.tile([P, w], F32, name=f"picked{i}_{r}")
+                nc.vector.tensor_tensor(
+                    out=picked[i, r][:],
+                    in0=y_all[:].indirect(lst[:, t0 // 16 : (t0 + w) // 16]),
+                    in1=gates[:, r, t0 : t0 + w],
+                    op=MULT,
+                )
+            if i >= 1:
+                finish(nc, keep, picked, out, i - 1, *pieces[i - 1])
+        finish(nc, keep, picked, out, len(pieces) - 1, *pieces[-1])
+
+
+def finish(nc, pool, picked, out, i, t0, w):
+    res = pool.tile([P, w], F32, name=f"res{i}")
+    nc.vector.tensor_tensor(out=res[:], in0=picked[i, 0][:], in1=picked[i, 1][:], op=ADD)
+    nc.sync.dma_start(out=out[:, t0 : t0 + w], in_=res[:])

@@ -50,19 +50,18 @@ def tile_moe_cap2_glu_silu_kernel(tc, xT, w1_words, w1_scales, w3_words, w3_scal
         gates = keep.tile([P, 2, T], F32, name="gates")
 
         x_raw = {}
-        x_grp = []
+        x_grp = {}
         x_codes = []
         x_bytes = []
-        g_codes = []
-        g_bytes = []
+        g_codes = {}
+        g_bytes = {}
         for s in range(PASSES):
             for c0, w in X_CHUNKS[s]:
-                x_raw[s, c0] = keep.tile([P, 4, w], F32, name=f"x_raw{s}_{c0}")
-            x_grp.append(keep.tile([P, T, 4], BF16, name=f"x_grp{s}", align_bytes=64))
+                x_raw[s, c0] = keep.tile([P, 4, w], F32, name=f"x_raw{s}_{c0}", tag=f"x_raw{s}_{c0}", align_bytes=64)
+            for c0, w in Q_CHUNKS[s]:
+                x_grp[s, c0] = keep.tile([P, w, 4], BF16, name=f"x_grp{s}_{c0}", tag=f"x_grp{s}_{c0}", align_bytes=64)
             x_codes.append(keep.tile([P, T], U32, name=f"x_codes{s}", align_bytes=64))
             x_bytes.append(keep.tile([P, T], U8, name=f"x_bytes{s}", align_bytes=64))
-            g_codes.append(keep.tile([P, S], U32, name=f"g_codes{s}", align_bytes=64))
-            g_bytes.append(keep.tile([P, S], U8, name=f"g_bytes{s}", align_bytes=64))
         y_all = keep.tile([P, S + PAD], F32, name="y_all")
         ident = keep.tile([P, P], F32, name="ident")
         warm = keep.tile([P, 1], F32, name="warm")
@@ -102,55 +101,60 @@ def tile_moe_cap2_glu_silu_kernel(tc, xT, w1_words, w1_scales, w3_words, w3_scal
 
         load_x_pass(0)
         nc.sync.dma_start(out=offs_t[:], in_=offs)
-        load_scales(nc.sync, w1_sc, w1_scales)
-        load_scales(nc.gpsimd, w3_sc, w3_scales)
         nc.gpsimd.memset(x_bytes[1][:].bitcast(I32), 0)
-        nc.gpsimd.memset(w2_sc[:].rearrange("p a b -> p (a b)").bitcast(I32), 0)
         nc.gpsimd.memset(y_all[:, S:], 0.0)
         make_identity(nc, ident[:])
-        load_scales(nc.gpsimd, w2_sc, w2_scales)
-        load_words(0)
+        nc.gpsimd.memset(w2_sc[:].rearrange("p a b -> p (a b)").bitcast(I32), 0)
         load_x_pass(1)
+        load_words(0)
+        load_scales(nc.sync, w1_sc, w1_scales)
+        load_scales(nc.sync, w3_sc, w3_scales)
         for e in range(1, E):
             load_words(e)
         load_w2()
+        load_scales(nc.sync, w2_sc, w2_scales)
         nc.sync.dma_start(out=pos1_t[:], in_=pos1)
         nc.sync.dma_start(out=pos2_t[:], in_=pos2)
         nc.sync.dma_start(out=gates[:], in_=gate.rearrange("r p t -> p r t"))
 
         def cast_x(s, c0, w):
             src = x_raw[s, c0][:].rearrange("p j c -> p c j")
+            dst = x_grp[s, c0]
             v = V_SHARE.get((s, c0), 0)
             if v:
-                nc.vector.tensor_copy(out=x_grp[s][:, c0 : c0 + v, :], in_=src[:, 0:v, :])
+                nc.vector.tensor_copy(out=dst[:, 0:v, :], in_=src[:, 0:v, :])
             if v < w:
-                nc.scalar.activation(out=x_grp[s][:, c0 + v : c0 + w, :], in_=src[:, v:w, :], func=COPY)
+                nc.scalar.activation(out=dst[:, v:w, :], in_=src[:, v:w, :], func=COPY)
 
         def quantize_x(s, c0, w):
             nc.vector.quantize_mx(
                 out=x_codes[s][:, c0 : c0 + w].bitcast(FP8X4),
                 scales=x_bytes[s][:, c0 : c0 + w],
-                in_=x_grp[s][:, c0 : c0 + w, :].rearrange("p c j -> p (c j)"),
+                in_=x_grp[s, c0][:].rearrange("p c j -> p (c j)"),
             )
 
-        def gather(s, e, n):
-            slots = slice(C * e, C * (e + n))
-            lst = offs_t[:, 16 * e : 16 * (e + n)]
-            nc.vector.tensor_copy(out=g_codes[s][:, slots], in_=x_codes[s][:].indirect(lst))
-            nc.vector.tensor_copy(out=g_bytes[s][:, slots], in_=x_bytes[s][:].indirect(lst))
+        follows = {(0, 2): ("x_grp1_512", "x_grp1_256"), (0, 3): ("x_grp1_0", "x_raw1_512")}
+
+        def gather(s, e):
+            lst = offs_t[:, 16 * e : 16 * (e + 1)]
+            t1, t2 = follows.get((s, e), (f"g_codes{s}_{e}", f"g_bytes{s}_{e}"))
+            g_codes[s, e] = keep.tile([P, C], U32, name=f"g_codes{s}_{e}", tag=t1, align_bytes=64)
+            g_bytes[s, e] = keep.tile([P, C], U8, name=f"g_bytes{s}_{e}", tag=t2, align_bytes=64)
+            nc.vector.tensor_copy(out=g_codes[s, e][:], in_=x_codes[s][:].indirect(lst))
+            nc.vector.tensor_copy(out=g_bytes[s, e][:], in_=x_bytes[s][:].indirect(lst))
 
         ab = {}
 
         def product(g, s):
             e = g // 2
-            cols = slice(P * g, P * (g + 1))
+            cols = slice(P * (g % 2), P * (g % 2 + 1))
             for m, wd, sc in ((0, w1_wd, w1_sc), (1, w3_wd, w3_sc)):
                 if s == 0:
                     ab[g, m] = banks.tile([P, H], F32, name="bank")
                 nc.tensor.matmul_mx(
                     out=ab[g, m][:],
-                    lhsT=g_codes[s][:, cols].bitcast(FP8X4),
-                    lhsT_scale=g_bytes[s][:, cols],
+                    lhsT=g_codes[s, e][:, cols].bitcast(FP8X4),
+                    lhsT_scale=g_bytes[s, e][:, cols],
                     rhs=wd[:, e, s, :].bitcast(FP4X4),
                     rhs_scale=sc[:, PASSES * e + s, :],
                     start=(s == 0),
@@ -214,19 +218,17 @@ def tile_moe_cap2_glu_silu_kernel(tc, xT, w1_words, w1_scales, w3_words, w3_scal
             cast_x(0, c0, w)
         for c0, w in Q_CHUNKS[0]:
             quantize_x(0, c0, w)
-        early = 3
-        gather(0, 0, 1)
-        gather(0, 1, 1)
-        for g in range(early):
-            product(g, 0)
+        gather(0, 0)
+        gather(0, 1)
+        product(0, 0)
+        product(1, 0)
         for c0, w in X_CHUNKS[1]:
             cast_x(1, c0, w)
-        gather(0, 2, 2)
         for c0, w in Q_CHUNKS[1]:
             quantize_x(1, c0, w)
 
         def stage_one(g):
-            if g >= early:
+            if g >= 2:
                 product(g, 0)
             product(g, 1)
             activate(g)
@@ -243,20 +245,23 @@ def tile_moe_cap2_glu_silu_kernel(tc, xT, w1_words, w1_scales, w3_words, w3_scal
         def finish_expert(e):
             second(grouped[e], e, C * e, C)
 
-        gather(1, 0, 1)
+        gather(1, 0)
         stage_one(0)
         stage_one(1)
-        gather(1, 1, 1)
+        gather(1, 1)
         stage_one(2)
         stage_one(3)
-        gather(1, 2, 2)
-        middle(0)
+        gather(0, 2)
+        gather(1, 2)
         stage_one(4)
         stage_one(5)
-        middle(1)
-        finish_expert(0)
+        middle(0)
+        gather(0, 3)
+        gather(1, 3)
         stage_one(6)
         stage_one(7)
+        middle(1)
+        finish_expert(0)
         middle(2)
         finish_expert(1)
         last = []

@@ -25,8 +25,8 @@ G = S // P
 
 FLOPS = 2 * S * (2 * K * H + H * N)
 
-X_CHUNKS = (((0, 512), (512, 256)), ((0, 256), (256, 256), (512, 256)))
-V_SHARE = {(0, 0): 288, (0, 512): 160}
+X_CHUNKS = (((0, 256), (256, 256), (512, 256)), ((0, 256), (256, 256), (512, 256)))
+V_SHARE = {(0, 0): 144, (0, 256): 144, (0, 512): 144, (1, 512): 128}
 Q_CHUNKS = (((0, 512), (512, 256)), ((0, 256), (256, 256), (512, 256)))
 
 
@@ -119,7 +119,8 @@ def tile_moe_cap2_glu_silu_kernel(tc, xT, w1_words, w1_scales, w3_words, w3_scal
 
         def cast_x(s, c0, w):
             src = x_raw[s, c0][:].rearrange("p j c -> p c j")
-            dst = x_grp[s, c0]
+            q0 = max(q for q, n in Q_CHUNKS[s] if q <= c0)
+            dst = x_grp[s, q0][:, c0 - q0 : c0 - q0 + w, :]
             v = V_SHARE.get((s, c0), 0)
             if v:
                 nc.vector.tensor_copy(out=dst[:, 0:v, :], in_=src[:, 0:v, :])
@@ -133,15 +134,23 @@ def tile_moe_cap2_glu_silu_kernel(tc, xT, w1_words, w1_scales, w3_words, w3_scal
                 in_=x_grp[s, c0][:].rearrange("p c j -> p (c j)"),
             )
 
-        follows = {(0, 2): ("x_grp1_512", "x_grp1_256"), (0, 3): ("x_grp1_0", "x_raw1_512")}
+        held = {}
 
         def gather(s, e):
             lst = offs_t[:, 16 * e : 16 * (e + 1)]
-            t1, t2 = follows.get((s, e), (f"g_codes{s}_{e}", f"g_bytes{s}_{e}"))
-            g_codes[s, e] = keep.tile([P, C], U32, name=f"g_codes{s}_{e}", tag=t1, align_bytes=64)
-            g_bytes[s, e] = keep.tile([P, C], U8, name=f"g_bytes{s}_{e}", tag=t2, align_bytes=64)
-            nc.vector.tensor_copy(out=g_codes[s, e][:], in_=x_codes[s][:].indirect(lst))
-            nc.vector.tensor_copy(out=g_bytes[s, e][:], in_=x_bytes[s][:].indirect(lst))
+            if (s, e) == (0, 2):
+                held["codes"] = keep.tile([P, 2, C], U32, name="late_codes", tag="x_grp1_512", align_bytes=64)
+                held["bytes"] = keep.tile([P, 2, C], U8, name="late_bytes", tag="x_raw1_512", align_bytes=64)
+            if s == 0 and e >= 2:
+                g_codes[s, e] = held["codes"][:, e - 2, :]
+                g_bytes[s, e] = held["bytes"][:, e - 2, :]
+            else:
+                codes = keep.tile([P, C], U32, name=f"g_codes{s}_{e}", align_bytes=64)
+                scales = keep.tile([P, C], U8, name=f"g_bytes{s}_{e}", align_bytes=64)
+                g_codes[s, e] = codes[:]
+                g_bytes[s, e] = scales[:]
+            nc.vector.tensor_copy(out=g_codes[s, e], in_=x_codes[s][:].indirect(lst))
+            nc.vector.tensor_copy(out=g_bytes[s, e], in_=x_bytes[s][:].indirect(lst))
 
         ab = {}
 
@@ -251,17 +260,17 @@ def tile_moe_cap2_glu_silu_kernel(tc, xT, w1_words, w1_scales, w3_words, w3_scal
         gather(1, 1)
         stage_one(2)
         stage_one(3)
+        middle(0)
         gather(0, 2)
         gather(1, 2)
         stage_one(4)
         stage_one(5)
-        middle(0)
+        middle(1)
+        finish_expert(0)
         gather(0, 3)
         gather(1, 3)
         stage_one(6)
         stage_one(7)
-        middle(1)
-        finish_expert(0)
         middle(2)
         finish_expert(1)
         last = []

from contextlib import ExitStack

import concourse.mybir as mybir
from concourse.masks import make_identity

F32 = mybir.dt.float32
BF16 = mybir.dt.bfloat16
I32 = mybir.dt.int32
U32 = mybir.dt.uint32
U16 = mybir.dt.uint16
U8 = mybir.dt.uint8
FP8X4 = mybir.dt.float8_e4m3fn_x4
FP4X4 = mybir.dt.float4_e2m1fn_x4
MULT = mybir.AluOpType.mult
ADD = mybir.AluOpType.add
COPY = mybir.ActivationFunctionType.Copy
SILU = mybir.ActivationFunctionType.Silu

K, T, E, C, H, N = 1024, 768, 4, 256, 512, 128
S = E * C
PAD = 32
P = 128
PASSES = K // 512
G = S // P

FLOPS = 2 * S * (2 * K * H + H * N)

X_CHUNKS = (((0, 256), (256, 256), (512, 256)), ((0, 256), (256, 256), (512, 256)))
V_SHARE = {(0, 0): 144, (0, 256): 144, (0, 512): 144, (1, 512): 128}
Q_CHUNKS = (((0, 512), (512, 256)), ((0, 256), (256, 256), (512, 256)))


def tile_moe_cap2_glu_silu_kernel(tc, xT, w1_words, w1_scales, w3_words, w3_scales, w2_words, w2_scales, gate, offs, pos1, pos2, out):
    nc = tc.nc
    with ExitStack() as ctx:
        keep = ctx.enter_context(tc.tile_pool(name="keep", bufs=1))
        work = ctx.enter_context(tc.tile_pool(name="work", bufs=4))
        banks = ctx.enter_context(tc.psum_pool(name="banks", bufs=8))

        offs_t = keep.tile([P, S // 16], U16, name="offs_t")
        pos1_t = keep.tile([P, T // 16], U16, name="pos1_t")
        pos2_t = keep.tile([P, T // 16], U16, name="pos2_t")

        w1_sc = keep.tile([P, E * PASSES, H], U8, name="w1_sc", align_bytes=64)
        w3_sc = keep.tile([P, E * PASSES, H], U8, name="w3_sc", align_bytes=64)
        w2_sc = keep.tile([P, E, N], U8, name="w2_sc", align_bytes=64)
        w1_wd = keep.tile([P, E, PASSES, 2 * H], U8, name="w1_wd", align_bytes=64)
        w3_wd = keep.tile([P, E, PASSES, 2 * H], U8, name="w3_wd", align_bytes=64)
        w2_wd = keep.tile([P, E, 2 * N], U8, name="w2_wd", align_bytes=64)
        gates = keep.tile([P, 2, T], F32, name="gates")

        x_raw = {}
        x_grp = {}
        x_codes = []
        x_bytes = []
        g_codes = {}
        g_bytes = {}
        for s in range(PASSES):
            for c0, w in X_CHUNKS[s]:
                x_raw[s, c0] = keep.tile([P, 4, w], F32, name=f"x_raw{s}_{c0}", tag=f"x_raw{s}_{c0}", align_bytes=64)
            for c0, w in Q_CHUNKS[s]:
                x_grp[s, c0] = keep.tile([P, w, 4], BF16, name=f"x_grp{s}_{c0}", tag=f"x_grp{s}_{c0}", align_bytes=64)
            x_codes.append(keep.tile([P, T], U32, name=f"x_codes{s}", align_bytes=64))
            x_bytes.append(keep.tile([P, T], U8, name=f"x_bytes{s}", align_bytes=64))
        y_all = keep.tile([P, S + PAD], F32, name="y_all")
        ident = keep.tile([P, P], F32, name="ident")
        warm = keep.tile([P, 1], F32, name="warm")

        nc.vector.memset(warm[:], 0.0)
        nc.scalar.activation(out=warm[:], in_=warm[:], func=SILU)
        nc.vector.memset(w1_sc[:].rearrange("p a b -> p (a b)").bitcast(I32), 0)
        nc.gpsimd.memset(w3_sc[:].rearrange("p a b -> p (a b)").bitcast(I32), 0)
        nc.gpsimd.memset(x_bytes[0][:].bitcast(I32), 0)

        def load_x(s, c0, w):
            rows = xT[512 * s : 512 * (s + 1), c0 : c0 + w].rearrange("(p j) c -> p j c", j=4)
            nc.sync.dma_start(out=x_raw[s, c0][:], in_=rows)

        def load_words(e):
            for tile, words in ((w1_wd, w1_words), (w3_wd, w3_words)):
                nc.sync.dma_start(
                    out=tile[:, e].bitcast(I32),
                    in_=words[e].rearrange("s p b -> p s b").bitcast(I32),
                )

        def load_scales(queue, tile, scales):
            for q in range(4):
                queue.dma_start(
                    out=tile[32 * q : 32 * q + 4].bitcast(I32),
                    in_=scales[:, :, 4 * q : 4 * q + 4, :].rearrange("e s r i -> r (e s) i").bitcast(I32),
                )

        def load_w2():
            nc.sync.dma_start(
                out=w2_wd[:].bitcast(I32), in_=w2_words.rearrange("e s p b -> p (e s) b").bitcast(I32)
            )

        def load_x_pass(s):
            for c0, w in X_CHUNKS[s]:
                load_x(s, c0, w)

        load_x_pass(0)
        nc.sync.dma_start(out=offs_t[:], in_=offs)
        nc.gpsimd.memset(x_bytes[1][:].bitcast(I32), 0)
        nc.gpsimd.memset(y_all[:, S:], 0.0)
        make_identity(nc, ident[:])
        nc.gpsimd.memset(w2_sc[:].rearrange("p a b -> p (a b)").bitcast(I32), 0)
        load_x_pass(1)
        load_words(0)
        load_scales(nc.sync, w1_sc, w1_scales)
        load_scales(nc.sync, w3_sc, w3_scales)
        for e in range(1, E):
            load_words(e)
        load_w2()
        load_scales(nc.sync, w2_sc, w2_scales)
        nc.sync.dma_start(out=pos1_t[:], in_=pos1)
        nc.sync.dma_start(out=pos2_t[:], in_=pos2)
        nc.sync.dma_start(out=gates[:], in_=gate.rearrange("r p t -> p r t"))

        def cast_x(s, c0, w):
            src = x_raw[s, c0][:].rearrange("p j c -> p c j")
            q0 = max(q for q, n in Q_CHUNKS[s] if q <= c0)
            dst = x_grp[s, q0][:, c0 - q0 : c0 - q0 + w, :]
            v = V_SHARE.get((s, c0), 0)
            if v:
                nc.vector.tensor_copy(out=dst[:, 0:v, :], in_=src[:, 0:v, :])
            if v < w:
                nc.scalar.activation(out=dst[:, v:w, :], in_=src[:, v:w, :], func=COPY)

        def quantize_x(s, c0, w):
            nc.vector.quantize_mx(
                out=x_codes[s][:, c0 : c0 + w].bitcast(FP8X4),
                scales=x_bytes[s][:, c0 : c0 + w],
                in_=x_grp[s, c0][:].rearrange("p c j -> p (c j)"),
            )

        held = {}

        def gather(s, e):
            lst = offs_t[:, 16 * e : 16 * (e + 1)]
            if (s, e) == (0, 2):
                held["codes"] = keep.tile([P, 2, C], U32, name="late_codes", tag="x_grp1_512", align_bytes=64)
                held["bytes"] = keep.tile([P, 2, C], U8, name="late_bytes", tag="x_raw1_512", align_bytes=64)
            if s == 0 and e >= 2:
                g_codes[s, e] = held["codes"][:, e - 2, :]
                g_bytes[s, e] = held["bytes"][:, e - 2, :]
            else:
                codes = keep.tile([P, C], U32, name=f"g_codes{s}_{e}", align_bytes=64)
                scales = keep.tile([P, C], U8, name=f"g_bytes{s}_{e}", align_bytes=64)
                g_codes[s, e] = codes[:]
                g_bytes[s, e] = scales[:]
            nc.vector.tensor_copy(out=g_codes[s, e], in_=x_codes[s][:].indirect(lst))
            nc.vector.tensor_copy(out=g_bytes[s, e], in_=x_bytes[s][:].indirect(lst))

        ab = {}

        def product(g, s):
            e = g // 2
            cols = slice(P * (g % 2), P * (g % 2 + 1))
            for m, wd, sc in ((0, w1_wd, w1_sc), (1, w3_wd, w3_sc)):
                if s == 0:
                    ab[g, m] = banks.tile([P, H], F32, name="bank")
                nc.tensor.matmul_mx(
                    out=ab[g, m][:],
                    lhsT=g_codes[s, e][:, cols].bitcast(FP8X4),
                    lhsT_scale=g_bytes[s, e][:, cols],
                    rhs=wd[:, e, s, :].bitcast(FP4X4),
                    rhs_scale=sc[:, PASSES * e + s, :],
                    start=(s == 0),
                    stop=(s == PASSES - 1),
                )

        sil = {}
        hid = {}

        def activate(g):
            sil[g] = work.tile([P, H], F32, name="sil")
            nc.scalar.activation(
                out=sil[g][:].rearrange("p (u m d) -> p u m d", u=2, d=2),
                in_=ab[g, 0][:].rearrange("p (m u d) -> p u m d", u=2, d=2),
                func=SILU,
            )

        def multiply(g):
            hid[g] = work.tile([P, H], BF16, name="hid")
            nc.vector.tensor_tensor(
                out=hid[g][:].rearrange("p (u m d) -> p u m d", u=2, d=2),
                in0=ab[g, 1][:].rearrange("p (m u d) -> p u m d", u=2, d=2),
                in1=sil[g][:].rearrange("p (u m d) -> p u m d", u=2, d=2),
                op=MULT,
            )

        def turn(bank, half, g):
            words = hid[g][:].bitcast(F32)
            for u in range(2):
                nc.tensor.transpose(bank[:, half, u, :], words[:, P * u : P * (u + 1)], ident[:])

        def unload(engine_copy, bank, n):
            grouped = work.tile([P, C, 4], BF16, name="grouped", align_bytes=64)
            engine_copy(
                out=grouped[:, 0 : P * n, :].rearrange("p c t -> p (c t)").bitcast(F32).rearrange("p (a c u) -> p a c u", a=n, u=2),
                in_=bank[:, 0:n, :, :].rearrange("p a u c -> p a c u"),
            )
            return grouped

        def second(grouped, e, c0, w):
            h_codes = work.tile([P, C], U32, name="h_codes", align_bytes=64)
            h_bytes = work.tile([P, C], U8, name="h_bytes", align_bytes=64)
            nc.vector.quantize_mx(
                out=h_codes[:, 0:w].bitcast(FP8X4),
                scales=h_bytes[:, 0:w],
                in_=grouped[:, 0:w, :].rearrange("p c t -> p (c t)"),
            )
            y = banks.tile([P, H], F32, name="bank")
            nc.tensor.matmul_mx(
                out=y[:, 0:w],
                lhsT=w2_wd[:, e, :].bitcast(FP4X4),
                lhsT_scale=w2_sc[:, e, :],
                rhs=h_codes[:, 0:w].bitcast(FP8X4),
                rhs_scale=h_bytes[:, 0:w],
                start=True,
                stop=True,
            )
            nc.scalar.copy(out=y_all[:, c0 : c0 + w], in_=y[:, 0:w])

        for c0, w in X_CHUNKS[0]:
            cast_x(0, c0, w)
        for c0, w in Q_CHUNKS[0]:
            quantize_x(0, c0, w)
        gather(0, 0)
        gather(0, 1)
        product(0, 0)
        product(1, 0)
        for c0, w in X_CHUNKS[1]:
            cast_x(1, c0, w)
        for c0, w in Q_CHUNKS[1]:
            quantize_x(1, c0, w)

        def stage_one(g):
            if g >= 2:
                product(g, 0)
            product(g, 1)
            activate(g)

        grouped = {}

        def middle(e):
            bank = banks.tile([P, 2, 2, P], F32, name="bank")
            for half in range(2):
                multiply(2 * e + half)
                turn(bank, half, 2 * e + half)
            grouped[e] = unload(nc.scalar.copy, bank, 2)

        def finish_expert(e):
            second(grouped[e], e, C * e, C)

        gather(1, 0)
        stage_one(0)
        stage_one(1)
        gather(1, 1)
        stage_one(2)
        stage_one(3)
        middle(0)
        gather(0, 2)
        gather(1, 2)
        stage_one(4)
        stage_one(5)
        middle(1)
        finish_expert(0)
        gather(0, 3)
        gather(1, 3)
        stage_one(6)
        stage_one(7)
        middle(2)
        finish_expert(1)
        last = []
        for half, engine_copy in ((0, nc.scalar.copy), (1, nc.vector.tensor_copy)):
            g = G - 2 + half
            bank = banks.tile([P, 2, 2, P], F32, name="bank")
            multiply(g)
            turn(bank, 0, g)
            last.append((engine_copy, bank, g))
        finish_expert(2)
        for engine_copy, bank, g in last:
            part = unload(engine_copy, bank, 1)
            second(part, E - 1, P * g, P)

        picked = {}
        pieces = ((0, 256), (256, 256), (512, 256))
        for i, (t0, w) in enumerate(pieces):
            for r, lst in ((0, pos1_t), (1, pos2_t)):
                picked[i, r] = keep.tile([P, w], F32, name=f"picked{i}_{r}")
                nc.vector.tensor_tensor(
                    out=picked[i, r][:],
                    in0=y_all[:].indirect(lst[:, t0 // 16 : (t0 + w) // 16]),
                    in1=gates[:, r, t0 : t0 + w],
                    op=MULT,
                )
            if i >= 1:
                finish(nc, keep, picked, out, i - 1, *pieces[i - 1])
        finish(nc, keep, picked, out, len(pieces) - 1, *pieces[-1])


def finish(nc, pool, picked, out, i, t0, w):
    res = pool.tile([P, w], F32, name=f"res{i}")
    nc.vector.tensor_tensor(out=res[:], in0=picked[i, 0][:], in1=picked[i, 1][:], op=ADD)
    nc.sync.dma_start(out=out[:, t0 : t0 + w], in_=res[:])
